import numpy as np
import ml_dtypes


def mxq(x, axis, fmt="e4m3"):
    dtype, down = {"e4m3": (ml_dtypes.float8_e4m3fn, 7), "e5m2": (ml_dtypes.float8_e5m2, 14)}[fmt]
    v = np.moveaxis(np.asarray(x, np.float32).astype(ml_dtypes.bfloat16).astype(np.float64), axis, -1)
    blocks = v.reshape(v.shape[:-1] + (-1, 32))
    amax = np.abs(blocks).max(-1, keepdims=True)
    byte = np.maximum(np.where(amax > 0, np.frexp(amax)[1] - 1 + 127, 0) - down, 1)
    scale = np.exp2(byte - 127.0)
    codes = (blocks / scale).astype(np.float32).astype(dtype).astype(np.float64)
    return np.moveaxis((codes * scale).reshape(v.shape), -1, axis)


WIDE = False


def mx_kscale(k):
    if not WIDE:
        return np.ones(k)
    levels = np.array([10, -10, 5, -5, 0])
    if k % 512:
        return np.exp2(np.random.permutation(np.resize(levels, k // 32))).repeat(32)
    a = np.empty((k // 512, 16))
    for p in range(k // 512):
        a[p, :8] = np.random.permutation(np.resize(levels, 8))
        for g in range(8):
            far = levels[np.abs(levels - a[p, g]) >= 10]
            a[p, g + 8] = far[np.random.randint(len(far))]
    return np.exp2(a.ravel()).repeat(32)


def f64(x):
    return np.asarray(x).astype(np.float64)


def striped(idx):
    return np.tile(idx.reshape(-1, 16).T, (8, 1)).astype(np.uint16)


def unstriped(offs):
    return offs[:16].T.reshape(-1).astype(np.int64)


def striped8(idx):
    return np.concatenate([x.reshape(-1, 16).T for x in idx]).astype(np.uint16)


def runs(offs, k):
    lists = np.stack([offs[16 * r : 16 * r + 16].T.reshape(-1) for r in range(8)]).astype(np.int64)
    return lists[np.arange(k) % 512 // 64]


def pack_weight(w):
    k, n = w.shape
    w = f64(np.asarray(w, np.float32).astype(ml_dtypes.bfloat16)).reshape(k // 32, 32, n)
    amax = np.abs(w).max(1)
    byte = np.clip(np.where(amax > 0, np.frexp(amax)[1] - 1 + 127 - 7, 1), 1, 254)
    scaled = (w * np.exp2(127.0 - byte)[:, None, :]).reshape(k, n).astype(np.float32)
    words = np.ascontiguousarray(scaled.reshape(k // 512, 128, 4, n).transpose(0, 1, 3, 2)).astype(ml_dtypes.float8_e4m3fn).view(np.uint8)
    return words, np.ascontiguousarray(byte.astype(np.uint8).reshape(k // 512, 16, n))


def unpack_weight(words, scales):
    g, p, n, _ = words.shape
    vals = np.ascontiguousarray(words).view(ml_dtypes.float8_e4m3fn).astype(np.float64) * np.repeat(np.exp2(scales.astype(np.float64) - 127.0), 8, axis=1)[..., None]
    return vals.transpose(0, 1, 3, 2).reshape(g * 512, n)


K, T, S, V, H, C = 512, 2048, 512, 512, 512, 256


def setup_inputs():
    n = np.random.standard_normal
    s = mx_kscale(K)[:, None]
    u = mx_kscale(S)
    packed_xT = pack_weight(n((K, T)) * s)
    return {
        "x_words": packed_xT[0],
        "x_scales": packed_xT[1],
        "w1": (n((K, H)) / np.sqrt(K) / s).astype(np.float32),
        "w2": (n((K, H)) / np.sqrt(K) / s).astype(np.float32),
        "ga": (np.random.uniform(0.5, 1.5, (H, 1)) * u[:, None]).astype(np.float32),
        "gb": (np.random.uniform(0.5, 1.5, (H, 1)) / u[:, None]).astype(np.float32),
        "offs": striped(np.random.permutation(T)[:S]),
        "two": striped(np.random.permutation(T)[:V]),
        "order": striped8(np.stack([np.random.permutation(S) for _ in range(8)])),
        "nq": striped8(np.stack([np.random.permutation(V) for _ in range(8)])),
    }


def reference(x_words, x_scales, w1, w2, ga, gb, offs, two, order, nq):
    xq = unpack_weight(x_words, x_scales)[:, unstriped(offs)]
    a = mxq(f64(w1), 0, "e4m3").T @ xq
    o = a[np.arange(H)[:, None], runs(order, H)]
    z = f64(ga) * (o.reshape(H, C, 2).max(axis=2))
    x_two = unpack_weight(x_words, x_scales)[:, unstriped(two)]
    b = mxq(f64(w2), 0, "e4m3").T @ x_two
    z2 = f64(gb) * (b - (b[np.arange(H)[:, None], runs(nq, H)]))
    s = 0.0625 * ((mxq(z, 0, "e4m3").T @ mxq(z2, 0, "e4m3")))
    return np.tanh(s)

@@ -1,0 +1,147 @@
+from contextlib import ExitStack
+
+import concourse.mybir as mybir
+
+F32 = mybir.dt.float32
+BF16 = mybir.dt.bfloat16
+I32 = mybir.dt.int32
+U32 = mybir.dt.uint32
+U16 = mybir.dt.uint16
+U8 = mybir.dt.uint8
+FP8X4 = mybir.dt.float8_e4m3fn_x4
+ALU = mybir.AluOpType
+ACT = mybir.ActivationFunctionType
+
+P = 128
+K, T, S, V, H, C = 512, 2048, 512, 512, 512, 256
+FLOPS = 2 * K * H * S + 2 * K * H * V + 2 * H * C * V
+
+
+def tile_picked_keypool_none_p_kernel(
+    tc, x_words, x_scales, w1, w2, ga, gb, offs, two, order, nq, out
+):
+    nc = tc.nc
+    with ExitStack() as ctx:
+        keep = ctx.enter_context(tc.tile_pool(name="keep", bufs=1))
+        psum = ctx.enter_context(tc.psum_pool(name="psum", bufs=1))
+
+        def sb(name, shape, dtype):
+            return keep.tile(shape, dtype, name=name, align_bytes=64)
+
+        def bank(n):
+            return psum.tile([P, 512], F32, name="bank%d" % n)
+
+        two_sb = sb("two_sb", [P, V // 16], U16)
+        offs_sb = sb("offs_sb", [P, S // 16], U16)
+        order_sb = sb("order_sb", [P, S // 16], U16)
+        nq_sb = sb("nq_sb", [P, V // 16], U16)
+        xw = sb("xw", [P, T], U32)
+        xs = sb("xs", [P, T], U8)
+        ga_sb = sb("ga_sb", [P, 4], F32)
+        gb_sb = sb("gb_sb", [P, 4], F32)
+        w1_raw = [sb("w1_raw%d" % h, [P, 4, 256], F32) for h in range(2)]
+        w2_raw = [sb("w2_raw%d" % h, [P, 4, 256], F32) for h in range(2)]
+
+        warm = sb("warm", [P, 1], F32)
+        nc.gpsimd.memset(warm[:], 0.0)
+        warm_out = sb("warm_out", [P, 1], F32)
+        nc.scalar.activation(warm_out[:], warm[:], ACT.Tanh)
+
+        nc.vector.memset(xs[:].bitcast(I32), 0)
+        nc.sync.dma_start(two_sb[:], two)
+        for q in range(4):
+            nc.scalar.dma_start(xs[32 * q : 32 * q + 4, :].bitcast(I32), x_scales[0, 4 * q : 4 * q + 4, :].bitcast(I32))
+        w2_rows = w2.rearrange("(p j) c -> p j c", j=4)
+        w1_rows = w1.rearrange("(p j) c -> p j c", j=4)
+        for h in range(2):
+            nc.sync.dma_start(w2_raw[h][:], w2_rows[:, :, 256 * h : 256 * h + 256])
+        nc.sync.dma_start(xw[:].bitcast(I32), x_words[0].rearrange("p c r -> p (c r)").bitcast(I32))
+        nc.sync.dma_start(offs_sb[:], offs)
+        nc.sync.dma_start(nq_sb[:], nq)
+        for h in range(2):
+            nc.sync.dma_start(w1_raw[h][:], w1_rows[:, :, 256 * h : 256 * h + 256])
+        nc.sync.dma_start(order_sb[:], order)
+        nc.gpsimd.dma_start(ga_sb[:], ga.rearrange("(p t) o -> p (t o)", t=4))
+        nc.gpsimd.dma_start(gb_sb[:], gb.rearrange("(p t) o -> p (t o)", t=4))
+
+        sgn01 = sb("sgn01", [P, 4], F32)
+        sgn = sb("sgn", [P, 4], F32)
+        ga_abs = sb("ga_abs", [P, 4], F32)
+        gb_sgn = sb("gb_sgn", [P, 4], F32)
+        nc.gpsimd.tensor_scalar(sgn01[:], ga_sb[:], 0.0, 2.0, ALU.is_ge, ALU.mult)
+        nc.gpsimd.tensor_scalar(sgn[:], sgn01[:], 1.0, -1.0, ALU.mult, ALU.add)
+        nc.gpsimd.tensor_tensor(ga_abs[:], ga_sb[:], sgn[:], ALU.mult)
+        nc.gpsimd.tensor_tensor(gb_sgn[:], gb_sb[:], sgn[:], ALU.mult)
+
+        def pick(name, lst):
+            words = sb(name + "_words", [P, 512], U32)
+            scales = sb(name + "_scales", [P, 512], U8)
+            nc.vector.tensor_copy(scales[:], xs[:].indirect(lst[:]))
+            nc.vector.tensor_copy(words[:], xw[:].indirect(lst[:]))
+            return words, scales
+
+        def quant(name, grouped, n):
+            codes = sb(name + "_codes", [P, n], U32)
+            scales = sb(name + "_sc", [P, n], U8)
+            nc.vector.quantize_mx(out=codes[:].bitcast(FP8X4), scales=scales[:], in_=grouped[:])
+            return codes, scales
+
+        def weights(name, raw):
+            grouped = sb(name + "_grouped", [P, 2048], BF16)
+            dst = grouped[:].rearrange("p (t m j) -> p m j t", t=4, j=4)
+            for h in range(2):
+                nc.scalar.copy(dst[:, 64 * h : 64 * h + 64], raw[h][:].rearrange("p j (m t) -> p m j t", t=4))
+            return quant(name, grouped, 512)
+
+        def project(name, wq, xq, gain, bank0):
+            rows = []
+            for t in range(4):
+                acc = bank(bank0 + t)
+                cols = slice(128 * t, 128 * t + 128)
+                nc.tensor.matmul_mx(
+                    out=acc[:], lhsT=wq[0][:, cols].bitcast(FP8X4), lhsT_scale=wq[1][:, cols],
+                    rhs=xq[0][:].bitcast(FP8X4), rhs_scale=xq[1][:], start=True, stop=True,
+                )
+                row = sb("%s%d" % (name, t), [P, 512], F32)
+                nc.scalar.activation(row[:], acc[:], ACT.Copy, scale=gain[:, t : t + 1])
+                rows.append(row)
+            return rows
+
+        w2q = weights("w2", w2_raw)
+        x_two = pick("x_two", two_sb)
+        b = project("b", w2q, x_two, gb_sgn, 0)
+        x_offs = pick("x_offs", offs_sb)
+        w1q = weights("w1", w1_raw)
+
+        z2_planes = sb("z2_planes", [P, 4, V], BF16)
+        for t in range(4):
+            got = sb("b_got%d" % t, [P, V], F32)
+            for h in range(2):
+                nc.vector.tensor_copy(got[:, 256 * h : 256 * h + 256], b[t][:].indirect(nq_sb[:, 16 * h : 16 * h + 16]))
+            nc.vector.tensor_tensor(z2_planes[:, t, :], b[t][:], got[:], ALU.subtract)
+        z2_grouped = sb("z2_grouped", [P, 4 * V], BF16)
+        nc.scalar.copy(
+            z2_grouped[:].rearrange("p (c i t) -> p c t i", i=4, t=4),
+            z2_planes[:].rearrange("p t (c i) -> p c t i", i=4),
+        )
+        a = project("a", w1q, x_offs, ga_abs, 4)
+        z2q = quant("z2", z2_grouped, 512)
+
+        for h in range(2):
+            got = sb("a_got%d" % h, [P, 4, 256], F32)
+            for t in range(4):
+                nc.vector.tensor_copy(got[:, t, :], a[t][:].indirect(order_sb[:, 16 * h : 16 * h + 16]))
+            z_grouped = sb("z_grouped%d" % h, [P, 512], BF16)
+            pairs = got[:].rearrange("p t (c i s) -> p c t i s", i=4, s=2)
+            nc.vector.tensor_tensor(
+                z_grouped[:].rearrange("p (c i t) -> p c t i", i=4, t=4), pairs[:, :, :, :, 0], pairs[:, :, :, :, 1], ALU.max
+            )
+            zq = quant("z%d" % h, z_grouped, 128)
+            acc = bank(h)
+            nc.tensor.matmul_mx(
+                out=acc[:], lhsT=zq[0][:].bitcast(FP8X4), lhsT_scale=zq[1][:],
+                rhs=z2q[0][:].bitcast(FP8X4), rhs_scale=z2q[1][:], start=True, stop=True,
+            )
+            res = sb("res%d" % h, [P, V], F32)
+            nc.scalar.activation(res[:], acc[:], ACT.Tanh, scale=0.0625)
+            nc.sync.dma_start(out[128 * h : 128 * h + 128, :], res[:])

@@ -25,8 +25,8 @@ def tile_picked_keypool_none_p_kernel(
         keep = ctx.enter_context(tc.tile_pool(name="keep", bufs=1))
         psum = ctx.enter_context(tc.psum_pool(name="psum", bufs=1))
 
-        def sb(name, shape, dtype):
-            return keep.tile(shape, dtype, name=name, align_bytes=64)
+        def sb(name, shape, dtype, tag=None):
+            return keep.tile(shape, dtype, name=name, tag=tag or name, align_bytes=64)
 
         def bank(n):
             return psum.tile([P, 512], F32, name="bank%d" % n)
@@ -37,41 +37,42 @@ def tile_picked_keypool_none_p_kernel(
         nq_sb = sb("nq_sb", [P, V // 16], U16)
         xw = sb("xw", [P, T], U32)
         xs = sb("xs", [P, T], U8)
-        ga_sb = sb("ga_sb", [P, 4], F32)
-        gb_sb = sb("gb_sb", [P, 4], F32)
-        w1_raw = [sb("w1_raw%d" % h, [P, 4, 256], F32) for h in range(2)]
-        w2_raw = [sb("w2_raw%d" % h, [P, 4, 256], F32) for h in range(2)]
+        gains = sb("gains", [P, 2, 8], F32)
 
+        nc.gpsimd.memset(xs[:].bitcast(I32), 0)
         warm = sb("warm", [P, 1], F32)
-        nc.gpsimd.memset(warm[:], 0.0)
+        nc.vector.memset(warm[:], 0.0)
         warm_out = sb("warm_out", [P, 1], F32)
         nc.scalar.activation(warm_out[:], warm[:], ACT.Tanh)
 
-        nc.vector.memset(xs[:].bitcast(I32), 0)
+        def load_weight(w):
+            rows = w.rearrange("(p j) c -> p j c", j=4)
+            raw = []
+            for h in range(2):
+                half = sb("w_raw%d" % h, [P, 4, 256], F32)
+                nc.sync.dma_start(half[:], rows[:, :, 256 * h : 256 * h + 256])
+                raw.append(half)
+            return raw
+
         nc.sync.dma_start(two_sb[:], two)
         for q in range(4):
-            nc.scalar.dma_start(xs[32 * q : 32 * q + 4, :].bitcast(I32), x_scales[0, 4 * q : 4 * q + 4, :].bitcast(I32))
-        w2_rows = w2.rearrange("(p j) c -> p j c", j=4)
-        w1_rows = w1.rearrange("(p j) c -> p j c", j=4)
-        for h in range(2):
-            nc.sync.dma_start(w2_raw[h][:], w2_rows[:, :, 256 * h : 256 * h + 256])
+            nc.sync.dma_start(xs[32 * q : 32 * q + 4, :].bitcast(I32), x_scales[0, 4 * q : 4 * q + 4, :].bitcast(I32))
+        w2_raw = load_weight(w2)
         nc.sync.dma_start(xw[:].bitcast(I32), x_words[0].rearrange("p c r -> p (c r)").bitcast(I32))
         nc.sync.dma_start(offs_sb[:], offs)
         nc.sync.dma_start(nq_sb[:], nq)
-        for h in range(2):
-            nc.sync.dma_start(w1_raw[h][:], w1_rows[:, :, 256 * h : 256 * h + 256])
         nc.sync.dma_start(order_sb[:], order)
-        nc.gpsimd.dma_start(ga_sb[:], ga.rearrange("(p t) o -> p (t o)", t=4))
-        nc.gpsimd.dma_start(gb_sb[:], gb.rearrange("(p t) o -> p (t o)", t=4))
+        nc.gpsimd.dma_start(gains[:, 0, 0:4], ga.rearrange("(p t) o -> p (t o)", t=4))
+        nc.gpsimd.dma_start(gains[:, 1, 0:4], gb.rearrange("(p t) o -> p (t o)", t=4))
 
-        sgn01 = sb("sgn01", [P, 4], F32)
-        sgn = sb("sgn", [P, 4], F32)
-        ga_abs = sb("ga_abs", [P, 4], F32)
-        gb_sgn = sb("gb_sgn", [P, 4], F32)
-        nc.gpsimd.tensor_scalar(sgn01[:], ga_sb[:], 0.0, 2.0, ALU.is_ge, ALU.mult)
-        nc.gpsimd.tensor_scalar(sgn[:], sgn01[:], 1.0, -1.0, ALU.mult, ALU.add)
-        nc.gpsimd.tensor_tensor(ga_abs[:], ga_sb[:], sgn[:], ALU.mult)
-        nc.gpsimd.tensor_tensor(gb_sgn[:], gb_sb[:], sgn[:], ALU.mult)
+        twice = sb("twice", [P, 4], F32)
+        sign = sb("sign", [P, 4], F32)
+        signed = sb("signed", [P, 2, 4], F32)
+        nc.gpsimd.tensor_scalar(twice[:], gains[:, 0, 0:4], 0.0, 2.0, ALU.is_ge, ALU.mult)
+        nc.gpsimd.tensor_scalar(sign[:], twice[:], 1.0, -1.0, ALU.mult, ALU.add)
+        nc.gpsimd.tensor_tensor(signed[:], gains[:, :, 0:4], sign[:].unsqueeze(1).to_broadcast([P, 2, 4]), ALU.mult)
+        ga_abs = signed[:, 0, :]
+        gb_sgn = signed[:, 1, :]
 
         def pick(name, lst):
             words = sb(name + "_words", [P, 512], U32)
@@ -86,62 +87,66 @@ def tile_picked_keypool_none_p_kernel(
             nc.vector.quantize_mx(out=codes[:].bitcast(FP8X4), scales=scales[:], in_=grouped[:])
             return codes, scales
 
-        def weights(name, raw):
-            grouped = sb(name + "_grouped", [P, 2048], BF16)
+        def deal(grouped, raw, h):
             dst = grouped[:].rearrange("p (t m j) -> p m j t", t=4, j=4)
-            for h in range(2):
-                nc.scalar.copy(dst[:, 64 * h : 64 * h + 64], raw[h][:].rearrange("p j (m t) -> p m j t", t=4))
-            return quant(name, grouped, 512)
+            nc.scalar.copy(dst[:, 64 * h : 64 * h + 64], raw[h][:].rearrange("p j (m t) -> p m j t", t=4))
 
-        def project(name, wq, xq, gain, bank0):
-            rows = []
-            for t in range(4):
-                acc = bank(bank0 + t)
-                cols = slice(128 * t, 128 * t + 128)
-                nc.tensor.matmul_mx(
-                    out=acc[:], lhsT=wq[0][:, cols].bitcast(FP8X4), lhsT_scale=wq[1][:, cols],
-                    rhs=xq[0][:].bitcast(FP8X4), rhs_scale=xq[1][:], start=True, stop=True,
-                )
-                row = sb("%s%d" % (name, t), [P, 512], F32)
-                nc.scalar.activation(row[:], acc[:], ACT.Copy, scale=gain[:, t : t + 1])
-                rows.append(row)
-            return rows
+        def project(name, wq, xq, gain, t, bank_no):
+            acc = bank(bank_no)
+            cols = slice(128 * t, 128 * t + 128)
+            nc.tensor.matmul_mx(
+                out=acc[:], lhsT=wq[0][:, cols].bitcast(FP8X4), lhsT_scale=wq[1][:, cols],
+                rhs=xq[0][:].bitcast(FP8X4), rhs_scale=xq[1][:], start=True, stop=True,
+            )
+            row = sb("%s%d" % (name, t), [P, 512], F32)
+            nc.scalar.activation(row[:], acc[:], ACT.Copy, scale=gain[:, t : t + 1])
+            return row
 
-        w2q = weights("w2", w2_raw)
+        w2_grouped = sb("w2_grouped", [P, 2048], BF16)
+        deal(w2_grouped, w2_raw, 0)
+        deal(w2_grouped, w2_raw, 1)
+        w2q = quant("w2", w2_grouped, 512)
         x_two = pick("x_two", two_sb)
-        b = project("b", w2q, x_two, gb_sgn, 0)
         x_offs = pick("x_offs", offs_sb)
-        w1q = weights("w1", w1_raw)
+        w1_raw = load_weight(w1)
+        w1_grouped = sb("w1_grouped", [P, 2048], BF16)
+        deal(w1_grouped, w1_raw, 0)
+        b = [project("b", w2q, x_two, gb_sgn, t, t) for t in range(2)]
+        deal(w1_grouped, w1_raw, 1)
+        b = b + [project("b", w2q, x_two, gb_sgn, t, t) for t in range(2, 4)]
+        w1q = quant("w1", w1_grouped, 512)
 
         z2_planes = sb("z2_planes", [P, 4, V], BF16)
         for t in range(4):
-            got = sb("b_got%d" % t, [P, V], F32)
+            got = sb("b_got%d" % t, [P, V], F32, tag="w1_grouped" if t == 2 else None)
             for h in range(2):
                 nc.vector.tensor_copy(got[:, 256 * h : 256 * h + 256], b[t][:].indirect(nq_sb[:, 16 * h : 16 * h + 16]))
-            nc.vector.tensor_tensor(z2_planes[:, t, :], b[t][:], got[:], ALU.subtract)
+            nc.gpsimd.tensor_tensor(z2_planes[:, t, :], b[t][:], got[:], ALU.subtract)
+        a = [project("a", w1q, x_offs, ga_abs, t, 4 + t) for t in range(4)]
         z2_grouped = sb("z2_grouped", [P, 4 * V], BF16)
         nc.scalar.copy(
             z2_grouped[:].rearrange("p (c i t) -> p c t i", i=4, t=4),
             z2_planes[:].rearrange("p t (c i) -> p c t i", i=4),
         )
-        a = project("a", w1q, x_offs, ga_abs, 4)
         z2q = quant("z2", z2_grouped, 512)
 
         for h in range(2):
             got = sb("a_got%d" % h, [P, 4, 256], F32)
             for t in range(4):
                 nc.vector.tensor_copy(got[:, t, :], a[t][:].indirect(order_sb[:, 16 * h : 16 * h + 16]))
-            z_grouped = sb("z_grouped%d" % h, [P, 512], BF16)
+            z_grouped = sb("z_grouped%d" % h, [P, 512], BF16, tag="z2_grouped" if h == 1 else None)
             pairs = got[:].rearrange("p t (c i s) -> p c t i s", i=4, s=2)
             nc.vector.tensor_tensor(
                 z_grouped[:].rearrange("p (c i t) -> p c t i", i=4, t=4), pairs[:, :, :, :, 0], pairs[:, :, :, :, 1], ALU.max
             )
             zq = quant("z%d" % h, z_grouped, 128)
-            acc = bank(h)
-            nc.tensor.matmul_mx(
-                out=acc[:], lhsT=zq[0][:].bitcast(FP8X4), lhsT_scale=zq[1][:],
-                rhs=z2q[0][:].bitcast(FP8X4), rhs_scale=z2q[1][:], start=True, stop=True,
-            )
-            res = sb("res%d" % h, [P, V], F32)
-            nc.scalar.activation(res[:], acc[:], ACT.Tanh, scale=0.0625)
-            nc.sync.dma_start(out[128 * h : 128 * h + 128, :], res[:])
+            for g in range(2):
+                cols = slice(256 * g, 256 * g + 256)
+                acc = bank(2 * h + g)
+                nc.tensor.matmul_mx(
+                    out=acc[:, 0:256], lhsT=zq[0][:].bitcast(FP8X4), lhsT_scale=zq[1][:],
+                    rhs=z2q[0][:, cols].bitcast(FP8X4), rhs_scale=z2q[1][:, cols], start=True, stop=True,
+                )
+                res = sb("res%d%d" % (h, g), [P, 256], F32)
+                nc.scalar.activation(res[:], acc[:, 0:256], ACT.Tanh, scale=0.0625)
+                nc.sync.dma_start(out[128 * h : 128 * h + 128, cols], res[:])

@@ -45,25 +45,23 @@ def tile_picked_keypool_none_p_kernel(
         warm_out = sb("warm_out", [P, 1], F32)
         nc.scalar.activation(warm_out[:], warm[:], ACT.Tanh)
 
-        def load_weight(w):
-            rows = w.rearrange("(p j) c -> p j c", j=4)
-            raw = []
-            for h in range(2):
-                half = sb("w_raw%d" % h, [P, 4, 256], F32)
-                nc.sync.dma_start(half[:], rows[:, :, 256 * h : 256 * h + 256])
-                raw.append(half)
-            return raw
+        def load_half(name, w, h):
+            half = sb("%s_raw%d" % (name, h), [P, 4, 256], F32)
+            nc.sync.dma_start(half[:], w.rearrange("(p j) c -> p j c", j=4)[:, :, 256 * h : 256 * h + 256])
+            return half
 
         nc.sync.dma_start(two_sb[:], two)
+        w2_raw = [load_half("w2", w2, 0)]
+        nc.sync.dma_start(offs_sb[:], offs)
         for q in range(4):
             nc.sync.dma_start(xs[32 * q : 32 * q + 4, :].bitcast(I32), x_scales[0, 4 * q : 4 * q + 4, :].bitcast(I32))
-        w2_raw = load_weight(w2)
+        w2_raw.append(load_half("w2", w2, 1))
         nc.sync.dma_start(xw[:].bitcast(I32), x_words[0].rearrange("p c r -> p (c r)").bitcast(I32))
-        nc.sync.dma_start(offs_sb[:], offs)
+        nc.sync.dma_start(gains[:, 0, 0:4], ga.rearrange("(p t) o -> p (t o)", t=4))
+        nc.sync.dma_start(gains[:, 1, 0:4], gb.rearrange("(p t) o -> p (t o)", t=4))
         nc.sync.dma_start(nq_sb[:], nq)
+        w1_raw = [load_half("w1", w1, h) for h in range(2)]
         nc.sync.dma_start(order_sb[:], order)
-        nc.gpsimd.dma_start(gains[:, 0, 0:4], ga.rearrange("(p t) o -> p (t o)", t=4))
-        nc.gpsimd.dma_start(gains[:, 1, 0:4], gb.rearrange("(p t) o -> p (t o)", t=4))
 
         twice = sb("twice", [P, 4], F32)
         sign = sb("sign", [P, 4], F32)
@@ -74,75 +72,101 @@ def tile_picked_keypool_none_p_kernel(
         ga_abs = signed[:, 0, :]
         gb_sgn = signed[:, 1, :]
 
-        def pick(name, lst):
-            words = sb(name + "_words", [P, 512], U32)
+        def pick_scales(name, lst):
             scales = sb(name + "_scales", [P, 512], U8)
             nc.vector.tensor_copy(scales[:], xs[:].indirect(lst[:]))
-            nc.vector.tensor_copy(words[:], xw[:].indirect(lst[:]))
+            return scales
+
+        def pick(name, lst, pieces, scales):
+            words = sb(name + "_words", [P, 512], U32)
+            n = 512 // pieces
+            for h in range(pieces):
+                nc.vector.tensor_copy(words[:, n * h : n * h + n], xw[:].indirect(lst[:, n // 16 * h : n // 16 * (h + 1)]))
             return words, scales
 
-        def quant(name, grouped, n):
+        def quant(name, grouped, n, pieces=1):
             codes = sb(name + "_codes", [P, n], U32)
             scales = sb(name + "_sc", [P, n], U8)
-            nc.vector.quantize_mx(out=codes[:].bitcast(FP8X4), scales=scales[:], in_=grouped[:])
+            m = n // pieces
+            for g in range(pieces):
+                nc.vector.quantize_mx(
+                    out=codes[:, m * g : m * g + m].bitcast(FP8X4), scales=scales[:, m * g : m * g + m],
+                    in_=grouped[:, 4 * m * g : 4 * m * (g + 1)],
+                )
             return codes, scales
 
-        def deal(grouped, raw, h):
+        def deal(grouped, raw, pieces, halves):
             dst = grouped[:].rearrange("p (t m j) -> p m j t", t=4, j=4)
-            nc.scalar.copy(dst[:, 64 * h : 64 * h + 64], raw[h][:].rearrange("p j (m t) -> p m j t", t=4))
+            n = 64 // pieces
+            for h in halves:
+                src = raw[h][:].rearrange("p j (m t) -> p m j t", t=4)
+                for m in range(0, 64, n):
+                    nc.scalar.copy(dst[:, 64 * h + m : 64 * h + m + n], src[:, m : m + n])
 
-        def project(name, wq, xq, gain, t, bank_no):
-            acc = bank(bank_no)
+        def project(row, wq, xq, gain, t, banks):
             cols = slice(128 * t, 128 * t + 128)
-            nc.tensor.matmul_mx(
-                out=acc[:], lhsT=wq[0][:, cols].bitcast(FP8X4), lhsT_scale=wq[1][:, cols],
-                rhs=xq[0][:].bitcast(FP8X4), rhs_scale=xq[1][:], start=True, stop=True,
-            )
-            row = sb("%s%d" % (name, t), [P, 512], F32)
-            nc.scalar.activation(row[:], acc[:], ACT.Copy, scale=gain[:, t : t + 1])
-            return row
+            n = 512 // len(banks)
+            for h, bank_no in enumerate(banks):
+                acc = bank(bank_no)
+                part = slice(n * h, n * h + n)
+                nc.tensor.matmul_mx(
+                    out=acc[:, 0:n], lhsT=wq[0][:, cols].bitcast(FP8X4), lhsT_scale=wq[1][:, cols],
+                    rhs=xq[0][:, part].bitcast(FP8X4), rhs_scale=xq[1][:, part], start=True, stop=True,
+                )
+                nc.scalar.activation(row[:, part], acc[:, 0:n], ACT.Copy, scale=gain[:, t : t + 1])
 
+        two_scales = pick_scales("x_two", two_sb)
+        offs_scales = pick_scales("x_offs", offs_sb)
         w2_grouped = sb("w2_grouped", [P, 2048], BF16)
-        deal(w2_grouped, w2_raw, 0)
-        deal(w2_grouped, w2_raw, 1)
+        deal(w2_grouped, w2_raw, 1, [0, 1])
         w2q = quant("w2", w2_grouped, 512)
-        x_two = pick("x_two", two_sb)
-        x_offs = pick("x_offs", offs_sb)
-        w1_raw = load_weight(w1)
+        x_two = pick("x_two", two_sb, 2, two_scales)
+        x_offs = pick("x_offs", offs_sb, 1, offs_scales)
         w1_grouped = sb("w1_grouped", [P, 2048], BF16)
-        deal(w1_grouped, w1_raw, 0)
-        b = [project("b", w2q, x_two, gb_sgn, t, t) for t in range(2)]
-        deal(w1_grouped, w1_raw, 1)
-        b = b + [project("b", w2q, x_two, gb_sgn, t, t) for t in range(2, 4)]
-        w1q = quant("w1", w1_grouped, 512)
+        b = [sb("b%d" % t, [P, 2 * V], F32) for t in range(4)]
+        nc.gpsimd.memset(b[0][:, V:], 0.0)
+        nc.gpsimd.memset(b[1][:, V:], 0.0)
+        project(b[0], w2q, x_two, gb_sgn, 0, [0, 1])
+        project(b[1], w2q, x_two, gb_sgn, 1, [2])
+        nc.gpsimd.tensor_scalar(
+            w1_grouped[:].rearrange("p (t m j) -> p m t j", t=4, j=4)[:, 0:64],
+            w1_raw[0][:].rearrange("p j (m t) -> p m t j", t=4), 1.0, 0.0, ALU.mult, ALU.add,
+        )
+        deal(w1_grouped, w1_raw, 1, [1])
+        project(b[2], w2q, x_two, gb_sgn, 2, [3])
+        project(b[3], w2q, x_two, gb_sgn, 3, [4])
+        w1q = quant("w1", w1_grouped, 512, 2)
 
         z2_planes = sb("z2_planes", [P, 4, V], BF16)
+        b_last = sb("b_last", [P, V], F32)
+        b_got = [b[2][:, V:], b[3][:, V:], b_last[:], w1_grouped[:, 0:1024].bitcast(F32)]
         for t in range(4):
-            got = sb("b_got%d" % t, [P, V], F32, tag="w1_grouped" if t == 2 else None)
-            for h in range(2):
-                nc.vector.tensor_copy(got[:, 256 * h : 256 * h + 256], b[t][:].indirect(nq_sb[:, 16 * h : 16 * h + 16]))
-            nc.gpsimd.tensor_tensor(z2_planes[:, t, :], b[t][:], got[:], ALU.subtract)
-        a = [project("a", w1q, x_offs, ga_abs, t, 4 + t) for t in range(4)]
+            got = b_got[t]
+            nc.vector.tensor_copy(got, b[t][:].indirect(nq_sb[:]))
+            nc.gpsimd.tensor_tensor(z2_planes[:, t, :], b[t][:, 0:V], got, ALU.subtract)
+        a = [sb("a%d" % t, [P, S], F32) for t in range(4)]
+        for t in range(4):
+            project(a[t], w1q, x_offs, ga_abs, t, [[5, 6], [7], [0], [1]][t])
         z2_grouped = sb("z2_grouped", [P, 4 * V], BF16)
         nc.scalar.copy(
             z2_grouped[:].rearrange("p (c i t) -> p c t i", i=4, t=4),
             z2_planes[:].rearrange("p t (c i) -> p c t i", i=4),
         )
-        z2q = quant("z2", z2_grouped, 512)
+        z2q = quant("z2", z2_grouped, 512, 2)
 
         for h in range(2):
             got = sb("a_got%d" % h, [P, 4, 256], F32)
             for t in range(4):
                 nc.vector.tensor_copy(got[:, t, :], a[t][:].indirect(order_sb[:, 16 * h : 16 * h + 16]))
-            z_grouped = sb("z_grouped%d" % h, [P, 512], BF16, tag="z2_grouped" if h == 1 else None)
+            z_grouped = z2_grouped[:, 0:512] if h == 1 else sb("z_grouped0", [P, 512], BF16)[:]
             pairs = got[:].rearrange("p t (c i s) -> p c t i s", i=4, s=2)
             nc.vector.tensor_tensor(
-                z_grouped[:].rearrange("p (c i t) -> p c t i", i=4, t=4), pairs[:, :, :, :, 0], pairs[:, :, :, :, 1], ALU.max
+                z_grouped.rearrange("p (c i t) -> p c t i", i=4, t=4), pairs[:, :, :, :, 0], pairs[:, :, :, :, 1], ALU.max
             )
             zq = quant("z%d" % h, z_grouped, 128)
             for g in range(2):
                 cols = slice(256 * g, 256 * g + 256)
-                acc = bank(2 * h + g)
+                acc = bank(2 + 2 * h + g)
                 nc.tensor.matmul_mx(
                     out=acc[:, 0:256], lhsT=zq[0][:].bitcast(FP8X4), lhsT_scale=zq[1][:],
                     rhs=z2q[0][:, cols].bitcast(FP8X4), rhs_scale=z2q[1][:, cols], start=True, stop=True,

@@ -13,8 +13,15 @@ ALU = mybir.AluOpType
 ACT = mybir.ActivationFunctionType
 
 P = 128
-K, T, S, V, H, C = 512, 2048, 512, 512, 512, 256
-FLOPS = 2 * K * H * S + 2 * K * H * V + 2 * H * C * V
+PACK = 4
+K, T, H = 512, 2048, 512
+N = 512
+C = N // 2
+HALF = N // 2
+LIST_COLS = N // 16
+GROUPED = PACK * N
+W1_GROUPS_ON_GPSIMD = 32
+FLOPS = 2 * K * H * N + 2 * K * H * N + 2 * H * C * N
 
 
 def tile_picked_keypool_none_p_kernel(
@@ -25,152 +32,170 @@ def tile_picked_keypool_none_p_kernel(
         keep = ctx.enter_context(tc.tile_pool(name="keep", bufs=1))
         psum = ctx.enter_context(tc.psum_pool(name="psum", bufs=1))
 
-        def sb(name, shape, dtype, tag=None):
-            return keep.tile(shape, dtype, name=name, tag=tag or name, align_bytes=64)
+        def sb(name, shape, dtype):
+            return keep.tile(shape, dtype, name=name, align_bytes=64)
 
-        def bank(n):
-            return psum.tile([P, 512], F32, name="bank%d" % n)
+        def bank(number):
+            return psum.tile([P, N], F32, name="bank%d" % number)
 
-        two_sb = sb("two_sb", [P, V // 16], U16)
-        offs_sb = sb("offs_sb", [P, S // 16], U16)
-        order_sb = sb("order_sb", [P, S // 16], U16)
-        nq_sb = sb("nq_sb", [P, V // 16], U16)
+        def half(h):
+            return slice(HALF * h, HALF * (h + 1))
+
+        two_sb = sb("two_sb", [P, LIST_COLS], U16)
+        offs_sb = sb("offs_sb", [P, LIST_COLS], U16)
+        order_sb = sb("order_sb", [P, LIST_COLS], U16)
+        nq_sb = sb("nq_sb", [P, LIST_COLS], U16)
         xw = sb("xw", [P, T], U32)
         xs = sb("xs", [P, T], U8)
         gains = sb("gains", [P, 2, 8], F32)
 
         nc.gpsimd.memset(xs[:].bitcast(I32), 0)
+
         warm = sb("warm", [P, 1], F32)
         nc.vector.memset(warm[:], 0.0)
         warm_out = sb("warm_out", [P, 1], F32)
         nc.scalar.activation(warm_out[:], warm[:], ACT.Tanh)
 
-        def load_half(name, w, h):
-            half = sb("%s_raw%d" % (name, h), [P, 4, 256], F32)
-            nc.sync.dma_start(half[:], w.rearrange("(p j) c -> p j c", j=4)[:, :, 256 * h : 256 * h + 256])
-            return half
+        def load_weight_half(name, w, h):
+            raw = sb("%s_raw%d" % (name, h), [P, PACK, HALF], F32)
+            nc.sync.dma_start(raw[:], w.rearrange("(p j) c -> p j c", j=PACK)[:, :, half(h)])
+            return raw
 
         nc.sync.dma_start(two_sb[:], two)
-        w2_raw = [load_half("w2", w2, 0)]
+        w2_raw = [load_weight_half("w2", w2, 0)]
         nc.sync.dma_start(offs_sb[:], offs)
         for q in range(4):
             nc.sync.dma_start(xs[32 * q : 32 * q + 4, :].bitcast(I32), x_scales[0, 4 * q : 4 * q + 4, :].bitcast(I32))
-        w2_raw.append(load_half("w2", w2, 1))
+        w2_raw.append(load_weight_half("w2", w2, 1))
         nc.sync.dma_start(xw[:].bitcast(I32), x_words[0].rearrange("p c r -> p (c r)").bitcast(I32))
-        nc.sync.dma_start(gains[:, 0, 0:4], ga.rearrange("(p t) o -> p (t o)", t=4))
-        nc.sync.dma_start(gains[:, 1, 0:4], gb.rearrange("(p t) o -> p (t o)", t=4))
+        nc.sync.dma_start(gains[:, 0, 0:PACK], ga.rearrange("(p t) o -> p (t o)", t=PACK))
+        nc.sync.dma_start(gains[:, 1, 0:PACK], gb.rearrange("(p t) o -> p (t o)", t=PACK))
         nc.sync.dma_start(nq_sb[:], nq)
-        w1_raw = [load_half("w1", w1, h) for h in range(2)]
+        w1_raw = [load_weight_half("w1", w1, h) for h in range(2)]
         nc.sync.dma_start(order_sb[:], order)
 
-        twice = sb("twice", [P, 4], F32)
-        sign = sb("sign", [P, 4], F32)
-        signed = sb("signed", [P, 2, 4], F32)
-        nc.gpsimd.tensor_scalar(twice[:], gains[:, 0, 0:4], 0.0, 2.0, ALU.is_ge, ALU.mult)
+        twice = sb("twice", [P, PACK], F32)
+        sign = sb("sign", [P, PACK], F32)
+        signed = sb("signed", [P, 2, PACK], F32)
+        nc.gpsimd.tensor_scalar(twice[:], gains[:, 0, 0:PACK], 0.0, 2.0, ALU.is_ge, ALU.mult)
         nc.gpsimd.tensor_scalar(sign[:], twice[:], 1.0, -1.0, ALU.mult, ALU.add)
-        nc.gpsimd.tensor_tensor(signed[:], gains[:, :, 0:4], sign[:].unsqueeze(1).to_broadcast([P, 2, 4]), ALU.mult)
+        nc.gpsimd.tensor_tensor(signed[:], gains[:, :, 0:PACK], sign[:].unsqueeze(1).to_broadcast([P, 2, PACK]), ALU.mult)
         ga_abs = signed[:, 0, :]
-        gb_sgn = signed[:, 1, :]
+        gb_signed = signed[:, 1, :]
 
-        def pick_scales(name, lst):
-            scales = sb(name + "_scales", [P, 512], U8)
-            nc.vector.tensor_copy(scales[:], xs[:].indirect(lst[:]))
+        def pick_scales(name, entries):
+            scales = sb(name + "_scales", [P, N], U8)
+            nc.vector.tensor_copy(scales[:], xs[:].indirect(entries[:]))
             return scales
 
-        def pick(name, lst, pieces, scales):
-            words = sb(name + "_words", [P, 512], U32)
-            n = 512 // pieces
-            for h in range(pieces):
-                nc.vector.tensor_copy(words[:, n * h : n * h + n], xw[:].indirect(lst[:, n // 16 * h : n // 16 * (h + 1)]))
-            return words, scales
+        def pick_words(name, entries, pieces):
+            words = sb(name + "_words", [P, N], U32)
+            n = N // pieces
+            for first in range(0, N, n):
+                nc.vector.tensor_copy(words[:, first : first + n], xw[:].indirect(entries[:, first // 16 : (first + n) // 16]))
+            return words
 
-        def quant(name, grouped, n, pieces=1):
-            codes = sb(name + "_codes", [P, n], U32)
-            scales = sb(name + "_sc", [P, n], U8)
-            m = n // pieces
-            for g in range(pieces):
+        def quantise(name, grouped, width, firsts):
+            codes = sb(name + "_codes", [P, width * len(firsts)], U32)
+            scales = sb(name + "_scales", [P, width * len(firsts)], U8)
+            for first in firsts:
                 nc.vector.quantize_mx(
-                    out=codes[:, m * g : m * g + m].bitcast(FP8X4), scales=scales[:, m * g : m * g + m],
-                    in_=grouped[:, 4 * m * g : 4 * m * (g + 1)],
+                    out=codes[:, first : first + width].bitcast(FP8X4),
+                    scales=scales[:, first : first + width],
+                    in_=grouped[:, PACK * first : PACK * (first + width)],
                 )
             return codes, scales
 
-        def deal(grouped, raw, pieces, halves):
-            dst = grouped[:].rearrange("p (t m j) -> p m j t", t=4, j=4)
-            n = 64 // pieces
-            for h in halves:
-                src = raw[h][:].rearrange("p j (m t) -> p m j t", t=4)
-                for m in range(0, 64, n):
-                    nc.scalar.copy(dst[:, 64 * h + m : 64 * h + m + n], src[:, m : m + n])
+        def deal_views(grouped, raw, h, first, walk):
+            dst = grouped.rearrange("p (t m j) -> p " + walk, t=PACK, j=PACK)
+            src = raw[h][:].rearrange("p j (m t) -> p " + walk, t=PACK)
+            return dst[:, P // 2 * h + first : P // 2 * (h + 1)], src[:, first:]
 
-        def project(row, wq, xq, gain, t, banks):
-            cols = slice(128 * t, 128 * t + 128)
-            n = 512 // len(banks)
-            for h, bank_no in enumerate(banks):
-                acc = bank(bank_no)
-                part = slice(n * h, n * h + n)
-                nc.tensor.matmul_mx(
-                    out=acc[:, 0:n], lhsT=wq[0][:, cols].bitcast(FP8X4), lhsT_scale=wq[1][:, cols],
-                    rhs=xq[0][:, part].bitcast(FP8X4), rhs_scale=xq[1][:, part], start=True, stop=True,
-                )
-                nc.scalar.activation(row[:, part], acc[:, 0:n], ACT.Copy, scale=gain[:, t : t + 1])
+        def deal_on_scalar(grouped, raw, h, first):
+            nc.scalar.copy(*deal_views(grouped, raw, h, first, "m j t"))
+
+        def product(acc, lhs, lhs_cols, rhs, rhs_cols):
+            nc.tensor.matmul_mx(
+                out=acc,
+                lhsT=lhs[0][:, lhs_cols].bitcast(FP8X4),
+                lhsT_scale=lhs[1][:, lhs_cols],
+                rhs=rhs[0][:, rhs_cols].bitcast(FP8X4),
+                rhs_scale=rhs[1][:, rhs_cols],
+                start=True,
+                stop=True,
+            )
+
+        def project(plane, w_mx, x_mx, gain, t, banks):
+            n = N // len(banks)
+            for piece, number in enumerate(banks):
+                acc = bank(number)
+                cols = slice(n * piece, n * (piece + 1))
+                product(acc[:, 0:n], w_mx, slice(P * t, P * (t + 1)), x_mx, cols)
+                nc.scalar.activation(plane[:, cols], acc[:, 0:n], ACT.Copy, scale=gain[:, t : t + 1])
 
         two_scales = pick_scales("x_two", two_sb)
         offs_scales = pick_scales("x_offs", offs_sb)
-        w2_grouped = sb("w2_grouped", [P, 2048], BF16)
-        deal(w2_grouped, w2_raw, 1, [0, 1])
-        w2q = quant("w2", w2_grouped, 512)
-        x_two = pick("x_two", two_sb, 2, two_scales)
-        x_offs = pick("x_offs", offs_sb, 1, offs_scales)
-        w1_grouped = sb("w1_grouped", [P, 2048], BF16)
-        b = [sb("b%d" % t, [P, 2 * V], F32) for t in range(4)]
-        nc.gpsimd.memset(b[0][:, V:], 0.0)
-        nc.gpsimd.memset(b[1][:, V:], 0.0)
-        project(b[0], w2q, x_two, gb_sgn, 0, [0, 1])
-        project(b[1], w2q, x_two, gb_sgn, 1, [2])
-        nc.gpsimd.tensor_scalar(
-            w1_grouped[:].rearrange("p (t m j) -> p m t j", t=4, j=4)[:, 0:64],
-            w1_raw[0][:].rearrange("p j (m t) -> p m t j", t=4), 1.0, 0.0, ALU.mult, ALU.add,
-        )
-        deal(w1_grouped, w1_raw, 1, [1])
-        project(b[2], w2q, x_two, gb_sgn, 2, [3])
-        project(b[3], w2q, x_two, gb_sgn, 3, [4])
-        w1q = quant("w1", w1_grouped, 512, 2)
-
-        z2_planes = sb("z2_planes", [P, 4, V], BF16)
-        b_last = sb("b_last", [P, V], F32)
-        b_got = [b[2][:, V:], b[3][:, V:], b_last[:], w1_grouped[:, 0:1024].bitcast(F32)]
-        for t in range(4):
-            got = b_got[t]
-            nc.vector.tensor_copy(got, b[t][:].indirect(nq_sb[:]))
-            nc.gpsimd.tensor_tensor(z2_planes[:, t, :], b[t][:, 0:V], got, ALU.subtract)
-        a = [sb("a%d" % t, [P, S], F32) for t in range(4)]
-        for t in range(4):
-            project(a[t], w1q, x_offs, ga_abs, t, [[5, 6], [7], [0], [1]][t])
-        z2_grouped = sb("z2_grouped", [P, 4 * V], BF16)
-        nc.scalar.copy(
-            z2_grouped[:].rearrange("p (c i t) -> p c t i", i=4, t=4),
-            z2_planes[:].rearrange("p t (c i) -> p c t i", i=4),
-        )
-        z2q = quant("z2", z2_grouped, 512, 2)
-
+        w2_grouped = sb("w2_grouped", [P, GROUPED], BF16)
         for h in range(2):
-            got = sb("a_got%d" % h, [P, 4, 256], F32)
-            for t in range(4):
-                nc.vector.tensor_copy(got[:, t, :], a[t][:].indirect(order_sb[:, 16 * h : 16 * h + 16]))
-            z_grouped = z2_grouped[:, 0:512] if h == 1 else sb("z_grouped0", [P, 512], BF16)[:]
-            pairs = got[:].rearrange("p t (c i s) -> p c t i s", i=4, s=2)
+            deal_on_scalar(w2_grouped[:], w2_raw, h, 0)
+        w2_mx = quantise("w2", w2_grouped, N, [0])
+        x_two = (pick_words("x_two", two_sb, 2), two_scales)
+        x_offs = (pick_words("x_offs", offs_sb, 1), offs_scales)
+
+        shared = sb("shared", [P, GROUPED + GROUPED // 2], BF16)
+        z2_planes = shared[:, 0:GROUPED].rearrange("p (t v) -> p t v", t=PACK)
+        w1_grouped = shared[:, GROUPED // 2 :]
+
+        b = [sb("b%d" % t, [P, 2 * N], F32) for t in range(PACK)]
+        for t in range(2):
+            nc.gpsimd.memset(b[t][:, N:], 0.0)
+        b_got = [b[2][:, N:], b[3][:, N:], sb("b_got2", [P, N], F32)[:], shared[:, GROUPED:].bitcast(F32)]
+
+        project(b[0], w2_mx, x_two, gb_signed, 0, [0, 1])
+        project(b[1], w2_mx, x_two, gb_signed, 1, [2])
+        dst, src = deal_views(w1_grouped, w1_raw, 0, 0, "m t j")
+        nc.gpsimd.tensor_scalar(
+            dst[:, 0:W1_GROUPS_ON_GPSIMD], src[:, 0:W1_GROUPS_ON_GPSIMD], 1.0, 0.0, ALU.mult, ALU.add
+        )
+        deal_on_scalar(w1_grouped, w1_raw, 0, W1_GROUPS_ON_GPSIMD)
+        deal_on_scalar(w1_grouped, w1_raw, 1, 0)
+        project(b[2], w2_mx, x_two, gb_signed, 2, [3])
+        project(b[3], w2_mx, x_two, gb_signed, 3, [4])
+        w1_mx = quantise("w1", w1_grouped, HALF, [HALF, 0])
+
+        for t in range(PACK):
+            nc.vector.tensor_copy(b_got[t], b[t][:].indirect(nq_sb[:]))
+            nc.gpsimd.tensor_tensor(z2_planes[:, t, :], b[t][:, 0:N], b_got[t], ALU.subtract)
+
+        a_order = [2, 3, 0, 1]
+        a = [sb("a%d" % t, [P, N], F32) for t in range(PACK)]
+        for t, banks in zip(a_order, [[5, 6], [7], [0], [1]]):
+            project(a[t], w1_mx, x_offs, ga_abs, t, banks)
+
+        z2_grouped = sb("z2_grouped", [P, GROUPED], BF16)
+        nc.scalar.copy(
+            z2_grouped[:].rearrange("p (c i t) -> p c t i", i=4, t=PACK),
+            z2_planes.rearrange("p t (c i) -> p c t i", i=4),
+        )
+        z2_mx = quantise("z2", z2_grouped, HALF, [0, HALF])
+
+        z_grouped = [sb("z_grouped0", [P, PACK * P], BF16)[:], z2_grouped[:, 0 : PACK * P]]
+        for h in range(2):
+            a_got = sb("a_got%d" % h, [P, PACK, HALF], F32)
+            for t in a_order:
+                entries = order_sb[:, LIST_COLS // 2 * h : LIST_COLS // 2 * (h + 1)]
+                nc.vector.tensor_copy(a_got[:, t, :], a[t][:].indirect(entries))
+            pairs = a_got[:].rearrange("p t (c i s) -> p c t i s", i=4, s=2)
             nc.vector.tensor_tensor(
-                z_grouped.rearrange("p (c i t) -> p c t i", i=4, t=4), pairs[:, :, :, :, 0], pairs[:, :, :, :, 1], ALU.max
+                z_grouped[h].rearrange("p (c i t) -> p c t i", i=4, t=PACK),
+                pairs[:, :, :, :, 0],
+                pairs[:, :, :, :, 1],
+                ALU.max,
             )
-            zq = quant("z%d" % h, z_grouped, 128)
+            z_mx = quantise("z%d" % h, z_grouped[h], P, [0])
             for g in range(2):
-                cols = slice(256 * g, 256 * g + 256)
                 acc = bank(2 + 2 * h + g)
-                nc.tensor.matmul_mx(
-                    out=acc[:, 0:256], lhsT=zq[0][:].bitcast(FP8X4), lhsT_scale=zq[1][:],
-                    rhs=z2q[0][:, cols].bitcast(FP8X4), rhs_scale=z2q[1][:, cols], start=True, stop=True,
-                )
-                res = sb("res%d%d" % (h, g), [P, 256], F32)
-                nc.scalar.activation(res[:], acc[:, 0:256], ACT.Tanh, scale=0.0625)
-                nc.sync.dma_start(out[128 * h : 128 * h + 128, cols], res[:])
+                product(acc[:, 0:HALF], z_mx, slice(0, P), z2_mx, half(g))
+                res = sb("res%d%d" % (h, g), [P, HALF], F32)
+                nc.scalar.activation(res[:], acc[:, 0:HALF], ACT.Tanh, scale=0.0625)
+                nc.sync.dma_start(out[P * h : P * (h + 1), half(g)], res[:])

from contextlib import ExitStack

import concourse.mybir as mybir

F32 = mybir.dt.float32
BF16 = mybir.dt.bfloat16
I32 = mybir.dt.int32
U32 = mybir.dt.uint32
U16 = mybir.dt.uint16
U8 = mybir.dt.uint8
FP8X4 = mybir.dt.float8_e4m3fn_x4
ALU = mybir.AluOpType
ACT = mybir.ActivationFunctionType

P = 128
PACK = 4
K, T, H = 512, 2048, 512
N = 512
C = N // 2
HALF = N // 2
LIST_COLS = N // 16
GROUPED = PACK * N
W1_GROUPS_ON_GPSIMD = 32
FLOPS = 2 * K * H * N + 2 * K * H * N + 2 * H * C * N


def tile_picked_keypool_none_p_kernel(
    tc, x_words, x_scales, w1, w2, ga, gb, offs, two, order, nq, out
):
    nc = tc.nc
    with ExitStack() as ctx:
        keep = ctx.enter_context(tc.tile_pool(name="keep", bufs=1))
        psum = ctx.enter_context(tc.psum_pool(name="psum", bufs=1))

        def sb(name, shape, dtype):
            return keep.tile(shape, dtype, name=name, align_bytes=64)

        def bank(number):
            return psum.tile([P, N], F32, name="bank%d" % number)

        def half(h):
            return slice(HALF * h, HALF * (h + 1))

        two_sb = sb("two_sb", [P, LIST_COLS], U16)
        offs_sb = sb("offs_sb", [P, LIST_COLS], U16)
        order_sb = sb("order_sb", [P, LIST_COLS], U16)
        nq_sb = sb("nq_sb", [P, LIST_COLS], U16)
        xw = sb("xw", [P, T], U32)
        xs = sb("xs", [P, T], U8)
        gains = sb("gains", [P, 2, 8], F32)

        nc.gpsimd.memset(xs[:].bitcast(I32), 0)

        warm = sb("warm", [P, 1], F32)
        nc.vector.memset(warm[:], 0.0)
        warm_out = sb("warm_out", [P, 1], F32)
        nc.scalar.activation(warm_out[:], warm[:], ACT.Tanh)

        def load_weight_half(name, w, h):
            raw = sb("%s_raw%d" % (name, h), [P, PACK, HALF], F32)
            nc.sync.dma_start(raw[:], w.rearrange("(p j) c -> p j c", j=PACK)[:, :, half(h)])
            return raw

        nc.sync.dma_start(two_sb[:], two)
        w2_raw = [load_weight_half("w2", w2, 0)]
        nc.sync.dma_start(offs_sb[:], offs)
        for q in range(4):
            nc.sync.dma_start(xs[32 * q : 32 * q + 4, :].bitcast(I32), x_scales[0, 4 * q : 4 * q + 4, :].bitcast(I32))
        w2_raw.append(load_weight_half("w2", w2, 1))
        nc.sync.dma_start(xw[:].bitcast(I32), x_words[0].rearrange("p c r -> p (c r)").bitcast(I32))
        nc.sync.dma_start(gains[:, 0, 0:PACK], ga.rearrange("(p t) o -> p (t o)", t=PACK))
        nc.sync.dma_start(gains[:, 1, 0:PACK], gb.rearrange("(p t) o -> p (t o)", t=PACK))
        nc.sync.dma_start(nq_sb[:], nq)
        w1_raw = [load_weight_half("w1", w1, h) for h in range(2)]
        nc.sync.dma_start(order_sb[:], order)

        twice = sb("twice", [P, PACK], F32)
        sign = sb("sign", [P, PACK], F32)
        signed = sb("signed", [P, 2, PACK], F32)
        nc.gpsimd.tensor_scalar(twice[:], gains[:, 0, 0:PACK], 0.0, 2.0, ALU.is_ge, ALU.mult)
        nc.gpsimd.tensor_scalar(sign[:], twice[:], 1.0, -1.0, ALU.mult, ALU.add)
        nc.gpsimd.tensor_tensor(signed[:], gains[:, :, 0:PACK], sign[:].unsqueeze(1).to_broadcast([P, 2, PACK]), ALU.mult)
        ga_abs = signed[:, 0, :]
        gb_signed = signed[:, 1, :]

        def pick_scales(name, entries):
            scales = sb(name + "_scales", [P, N], U8)
            nc.vector.tensor_copy(scales[:], xs[:].indirect(entries[:]))
            return scales

        def pick_words(name, entries, pieces):
            words = sb(name + "_words", [P, N], U32)
            n = N // pieces
            for first in range(0, N, n):
                nc.vector.tensor_copy(words[:, first : first + n], xw[:].indirect(entries[:, first // 16 : (first + n) // 16]))
            return words

        def quantise(name, grouped, width, firsts):
            codes = sb(name + "_codes", [P, width * len(firsts)], U32)
            scales = sb(name + "_scales", [P, width * len(firsts)], U8)
            for first in firsts:
                nc.vector.quantize_mx(
                    out=codes[:, first : first + width].bitcast(FP8X4),
                    scales=scales[:, first : first + width],
                    in_=grouped[:, PACK * first : PACK * (first + width)],
                )
            return codes, scales

        def deal_views(grouped, raw, h, first, walk):
            dst = grouped.rearrange("p (t m j) -> p " + walk, t=PACK, j=PACK)
            src = raw[h][:].rearrange("p j (m t) -> p " + walk, t=PACK)
            return dst[:, P // 2 * h + first : P // 2 * (h + 1)], src[:, first:]

        def deal_on_scalar(grouped, raw, h, first):
            nc.scalar.copy(*deal_views(grouped, raw, h, first, "m j t"))

        def product(acc, lhs, lhs_cols, rhs, rhs_cols):
            nc.tensor.matmul_mx(
                out=acc,
                lhsT=lhs[0][:, lhs_cols].bitcast(FP8X4),
                lhsT_scale=lhs[1][:, lhs_cols],
                rhs=rhs[0][:, rhs_cols].bitcast(FP8X4),
                rhs_scale=rhs[1][:, rhs_cols],
                start=True,
                stop=True,
            )

        def project(plane, w_mx, x_mx, gain, t, banks):
            n = N // len(banks)
            for piece, number in enumerate(banks):
                acc = bank(number)
                cols = slice(n * piece, n * (piece + 1))
                product(acc[:, 0:n], w_mx, slice(P * t, P * (t + 1)), x_mx, cols)
                nc.scalar.activation(plane[:, cols], acc[:, 0:n], ACT.Copy, scale=gain[:, t : t + 1])

        two_scales = pick_scales("x_two", two_sb)
        offs_scales = pick_scales("x_offs", offs_sb)
        w2_grouped = sb("w2_grouped", [P, GROUPED], BF16)
        for h in range(2):
            deal_on_scalar(w2_grouped[:], w2_raw, h, 0)
        w2_mx = quantise("w2", w2_grouped, N, [0])
        x_two = (pick_words("x_two", two_sb, 2), two_scales)
        x_offs = (pick_words("x_offs", offs_sb, 1), offs_scales)

        shared = sb("shared", [P, GROUPED + GROUPED // 2], BF16)
        z2_planes = shared[:, 0:GROUPED].rearrange("p (t v) -> p t v", t=PACK)
        w1_grouped = shared[:, GROUPED // 2 :]

        b = [sb("b%d" % t, [P, 2 * N], F32) for t in range(PACK)]
        for t in range(2):
            nc.gpsimd.memset(b[t][:, N:], 0.0)
        b_got = [b[2][:, N:], b[3][:, N:], sb("b_got2", [P, N], F32)[:], shared[:, GROUPED:].bitcast(F32)]

        project(b[0], w2_mx, x_two, gb_signed, 0, [0, 1])
        project(b[1], w2_mx, x_two, gb_signed, 1, [2])
        dst, src = deal_views(w1_grouped, w1_raw, 0, 0, "m t j")
        nc.gpsimd.tensor_scalar(
            dst[:, 0:W1_GROUPS_ON_GPSIMD], src[:, 0:W1_GROUPS_ON_GPSIMD], 1.0, 0.0, ALU.mult, ALU.add
        )
        deal_on_scalar(w1_grouped, w1_raw, 0, W1_GROUPS_ON_GPSIMD)
        deal_on_scalar(w1_grouped, w1_raw, 1, 0)
        project(b[2], w2_mx, x_two, gb_signed, 2, [3])
        project(b[3], w2_mx, x_two, gb_signed, 3, [4])
        w1_mx = quantise("w1", w1_grouped, HALF, [HALF, 0])

        for t in range(PACK):
            nc.vector.tensor_copy(b_got[t], b[t][:].indirect(nq_sb[:]))
            nc.gpsimd.tensor_tensor(z2_planes[:, t, :], b[t][:, 0:N], b_got[t], ALU.subtract)

        a_order = [2, 3, 0, 1]
        a = [sb("a%d" % t, [P, N], F32) for t in range(PACK)]
        for t, banks in zip(a_order, [[5, 6], [7], [0], [1]]):
            project(a[t], w1_mx, x_offs, ga_abs, t, banks)

        z2_grouped = sb("z2_grouped", [P, GROUPED], BF16)
        nc.scalar.copy(
            z2_grouped[:].rearrange("p (c i t) -> p c t i", i=4, t=PACK),
            z2_planes.rearrange("p t (c i) -> p c t i", i=4),
        )
        z2_mx = quantise("z2", z2_grouped, HALF, [0, HALF])

        z_grouped = [sb("z_grouped0", [P, PACK * P], BF16)[:], z2_grouped[:, 0 : PACK * P]]
        for h in range(2):
            a_got = sb("a_got%d" % h, [P, PACK, HALF], F32)
            for t in a_order:
                entries = order_sb[:, LIST_COLS // 2 * h : LIST_COLS // 2 * (h + 1)]
                nc.vector.tensor_copy(a_got[:, t, :], a[t][:].indirect(entries))
            pairs = a_got[:].rearrange("p t (c i s) -> p c t i s", i=4, s=2)
            nc.vector.tensor_tensor(
                z_grouped[h].rearrange("p (c i t) -> p c t i", i=4, t=PACK),
                pairs[:, :, :, :, 0],
                pairs[:, :, :, :, 1],
                ALU.max,
            )
            z_mx = quantise("z%d" % h, z_grouped[h], P, [0])
            for g in range(2):
                acc = bank(2 + 2 * h + g)
                product(acc[:, 0:HALF], z_mx, slice(0, P), z2_mx, half(g))
                res = sb("res%d%d" % (h, g), [P, HALF], F32)
                nc.scalar.activation(res[:], acc[:, 0:HALF], ACT.Tanh, scale=0.0625)
                nc.sync.dma_start(out[P * h : P * (h + 1), half(g)], res[:])
